import numpy as np
import ml_dtypes


def mxq(x, axis, fmt="e4m3"):
    dtype, down = {"e4m3": (ml_dtypes.float8_e4m3fn, 7), "e5m2": (ml_dtypes.float8_e5m2, 14)}[fmt]
    v = np.moveaxis(np.asarray(x, np.float32).astype(ml_dtypes.bfloat16).astype(np.float64), axis, -1)
    blocks = v.reshape(v.shape[:-1] + (-1, 32))
    amax = np.abs(blocks).max(-1, keepdims=True)
    byte = np.maximum(np.where(amax > 0, np.frexp(amax)[1] - 1 + 127, 0) - down, 1)
    scale = np.exp2(byte - 127.0)
    codes = (blocks / scale).astype(np.float32).astype(dtype).astype(np.float64)
    return np.moveaxis((codes * scale).reshape(v.shape), -1, axis)


WIDE = False


def mx_kscale(k):
    if not WIDE:
        return np.ones(k)
    levels = np.array([10, -10, 5, -5, 0])
    if k % 512:
        return np.exp2(np.random.permutation(np.resize(levels, k // 32))).repeat(32)
    a = np.empty((k // 512, 16))
    for p in range(k // 512):
        a[p, :8] = np.random.permutation(np.resize(levels, 8))
        for g in range(8):
            far = levels[np.abs(levels - a[p, g]) >= 10]
            a[p, g + 8] = far[np.random.randint(len(far))]
    return np.exp2(a.ravel()).repeat(32)


BF16 = ml_dtypes.bfloat16


def bf(x):
    return np.asarray(x, np.float32).astype(BF16)


def f64(x):
    return np.asarray(x).astype(np.float64)


E2M1 = np.array([0.0, 0.5, 1.0, 1.5, 2.0, 3.0, 4.0, 6.0, -0.0, -0.5, -1.0, -1.5, -2.0, -3.0, -4.0, -6.0])


def pack_weight(w, fmt):
    k, n = w.shape
    w = f64(bf(w)).reshape(k // 32, 32, n)
    amax = np.abs(w).max(1)
    if fmt == "e4m3":
        byte = np.frexp(amax)[1] - 1 + 127 - 7
    else:
        mant, ex = np.frexp(amax / 6.0)
        byte = np.where(mant > 0.5, ex, ex - 1) + 127
    byte = np.clip(np.where(amax > 0, byte, 1), 1, 254)
    scaled = (w * np.exp2(127.0 - byte)[:, None, :]).reshape(k, n).astype(np.float32)
    by_word = np.ascontiguousarray(scaled.reshape(k // 512, 128, 4, n).transpose(0, 1, 3, 2))
    if fmt == "e4m3":
        words = by_word.astype(ml_dtypes.float8_e4m3fn).view(np.uint8)
    else:
        c = by_word.astype(ml_dtypes.float4_e2m1fn).view(np.uint8) & 0xF
        words = c[..., 0::2] | (c[..., 1::2] << 4)
    return np.ascontiguousarray(words), np.ascontiguousarray(byte.astype(np.uint8).reshape(k // 512, 16, n))


def unpack_weight(words, scales, fmt):
    g, p, n, _ = words.shape
    if fmt == "e4m3":
        vals = np.ascontiguousarray(words).view(ml_dtypes.float8_e4m3fn).astype(np.float64)
    else:
        nib = np.empty((g, p, n, 4), np.uint8)
        nib[..., 0::2] = words & 0xF
        nib[..., 1::2] = words >> 4
        vals = E2M1[nib]
    vals = vals * np.repeat(np.exp2(scales.astype(np.float64) - 127.0), 8, axis=1)[..., None]
    return vals.transpose(0, 1, 3, 2).reshape(g * 512, n)
def pack4(w):
    words, scales = pack_weight(w, "e2m1")
    return words.reshape(words.shape[0], 128, -1), scales


def unpack4(words, scales):
    return unpack_weight(words.reshape(words.shape[0], 128, -1, 2), scales, "e2m1")


M, K, V, D, R = 1024, 1024, 1536, 512, 512


def setup_inputs():
    s, t, u = mx_kscale(K), mx_kscale(V), mx_kscale(M)
    x = np.random.standard_normal((M, K)) * s * u[:, None]
    w_pi = np.random.standard_normal((K, V)) / np.sqrt(K) / s[:, None] * t
    w_act = np.random.standard_normal((K, V)) / np.sqrt(K) / s[:, None]
    beta = (1 + 0.1 * np.random.standard_normal(V)) * t
    values = 0.5 * np.random.standard_normal(M) * u
    e_words, e_scales = pack4(np.random.standard_normal((V, D)) / np.sqrt(V) / t[:, None])
    mix = np.random.standard_normal((R, M)) / np.sqrt(M) / u
    return {"x": bf(x), "w_pi": bf(w_pi), "w_act": bf(w_act), "beta": bf(beta),
            "values": bf(values), "e_words": e_words, "e_scales": e_scales, "mix": bf(mix)}


def reference(x, w_pi, w_act, beta, values, e_words, e_scales, mix):
    xq = mxq(f64(x), 1, "e4m3")
    policy = xq @ mxq(f64(w_pi), 0, "e4m3")
    action = xq @ mxq(f64(w_act), 0, "e4m3")
    score = policy + f64(beta) * (action - f64(values)[:, None])
    sketch = mxq(score, 1, "e4m3") @ unpack4(e_words, e_scales)
    mixed = mxq(f64(mix), 1, "e4m3") @ mxq(score, 0, "e4m3")
    return sketch, mixed

@@ -1,0 +1,458 @@
+from contextlib import ExitStack
+
+import concourse.mybir as mybir
+from concourse.masks import make_identity
+
+M, K, V, D, R = 1024, 1024, 1536, 512, 512
+FLOPS = 2 * (2 * M * K * V + M * V * D + R * M * V)
+
+F32 = mybir.dt.float32
+BF16 = mybir.dt.bfloat16
+I32 = mybir.dt.int32
+U32 = mybir.dt.uint32
+U8 = mybir.dt.uint8
+FP8X4 = mybir.dt.float8_e4m3fn_x4
+FP4X4 = mybir.dt.float4_e2m1fn_x4
+ALU = mybir.AluOpType
+
+P = 128
+PACK = 4
+PASS = P * PACK
+GROUPS = M // PASS
+CHUNKS = V // PASS
+KPASSES = K // PASS
+RTILES = R // P
+ORDER = [(0, 0), (0, 1), (1, 0), (1, 1), (2, 0), (2, 1)]
+W_SLOT = [0, 1, 2, 3, 1, 2, 3, 0, 1, 0, 2, 3]
+C_SLOT = [3, 1, 4, 5, 0, 1]
+X_HALF = [8, 9, 10, 11, 0, 1, 3, 2]
+
+
+def tile_ilql_score_sketch_mix_s8_kernel(
+    tc, x, w_pi, w_act, beta, values, e_words, e_scales, mix, sketch, mixed
+):
+    nc = tc.nc
+    with ExitStack() as ctx:
+        sb = ctx.enter_context(tc.tile_pool(name="sb", bufs=1))
+        ps = ctx.enter_context(tc.psum_pool(name="ps", bufs=1))
+
+        def tiles(name, count, width, dtype):
+            return [sb.tile([P, width], dtype, name="%s%d" % (name, i), align_bytes=64) for i in range(count)]
+
+        banks = [ps.tile([P, PASS], F32, name="bank%d" % i) for i in range(8)]
+
+        ident = sb.tile([P, P], F32, name="ident")
+        beta_words = sb.tile([P, CHUNKS * PACK], BF16, name="beta_words")
+        value_cols = sb.tile([P, GROUPS * PACK], BF16, name="value_cols")
+        beta_rows = tiles("beta_rows", CHUNKS, PASS, BF16)
+        x_raw = tiles("x_raw", GROUPS * PACK, K, BF16)
+        x_codes = tiles("x_codes", GROUPS * PACK, KPASSES * P, U32)
+        x_scales = tiles("x_scales", GROUPS * PACK, KPASSES * P, U8)
+        mix_raw = x_raw[:RTILES]
+        mix_codes = tiles("mix_codes", RTILES, GROUPS * P, U32)
+        mix_scales = tiles("mix_scales", RTILES, GROUPS * P, U8)
+        n_pieces = CHUNKS * 2 * KPASSES
+        w_raw = tiles("w_raw", n_pieces, PACK * PASS, BF16)
+        w_laid = tiles("w_laid", 6, PACK * PASS, BF16)
+        w_codes = tiles("w_codes", n_pieces, PASS, U32)
+        w_scales = tiles("w_scales", n_pieces, PASS, U8)
+        e_codes = sb.tile([P, CHUNKS * 2 * D], U8, name="e_codes", align_bytes=64)
+        e_plane = sb.tile([P, CHUNKS * D], U8, name="e_plane", align_bytes=64)
+        advantage = tiles("advantage", 4, PASS, F32)
+        score = tiles("score", 3, PACK * PASS, BF16)
+        by_token = w_raw
+        by_context = [w_laid[s] for s in C_SLOT]
+        n_blocks = CHUNKS * GROUPS
+        tok_codes = tiles("tok_codes", n_blocks, PASS, U32)
+        tok_scales = tiles("tok_scales", n_blocks, PASS, U8)
+        ctx_codes = tiles("ctx_codes", n_blocks, PASS, U32)
+        ctx_scales = tiles("ctx_scales", n_blocks, PASS, U8)
+        result = tiles("result", 8, PASS, F32)
+
+        def copy_on(engine, out, in_):
+            if engine == "vector":
+                nc.vector.tensor_copy(out=out, in_=in_)
+            elif engine == "scalar":
+                nc.scalar.copy(out=out, in_=in_)
+            else:
+                nc.gpsimd.tensor_scalar(out=out, in0=in_, scalar1=1.0, scalar2=0.0, op0=ALU.mult, op1=ALU.add)
+
+        def quantize(codes, scales, laid):
+            nc.vector.quantize_mx(out=codes[:].bitcast(FP8X4), scales=scales[:], in_=laid[:])
+
+        def half(h):
+            return w_laid[h // 2][:, (h % 2) * K : (h % 2 + 1) * K]
+
+        x_rows = x.rearrange("(g p t) k -> g t p k", p=P, t=PACK)
+        sketch_rows = sketch.rearrange("(g p t) d -> g t p d", p=P, t=PACK)
+
+        def load_x(i):
+            nc.sync.dma_start(out=x_raw[i][:], in_=x_rows[i // PACK, i % PACK])
+
+        def load_mix(i):
+            nc.sync.dma_start(out=mix_raw[i][:], in_=mix[i * P : (i + 1) * P, :])
+
+        def piece(c, which, kk):
+            return (c * 2 + which) * KPASSES + kk
+
+        def load_w(i):
+            c, which, kk = i // (2 * KPASSES), (i // KPASSES) % 2, i % KPASSES
+            src = (w_act, w_pi)[which][kk * PASS : (kk + 1) * PASS, c * PASS : (c + 1) * PASS]
+            nc.sync.dma_start(
+                out=w_raw[i][:].rearrange("p (j n) -> p j n", j=PACK),
+                in_=src.rearrange("(p j) n -> p j n", j=PACK),
+            )
+
+        def load_small():
+            nc.scalar.dma_start(
+                out=beta_words[:].rearrange("a (c f) -> a c f", f=PACK),
+                in_=beta.rearrange("(c a f) -> a c f", a=P, f=PACK),
+            )
+            nc.scalar.dma_start(
+                out=value_cols[:].rearrange("p (g t) -> p g t", t=PACK),
+                in_=values.rearrange("(g p t) -> p g t", p=P, t=PACK),
+            )
+
+        def load_e():
+            nc.sync.dma_start(
+                out=e_codes[:].bitcast(I32).rearrange("p (c w) -> p c w", c=CHUNKS),
+                in_=e_words.bitcast(I32).rearrange("c p w -> p c w"),
+            )
+            rows = e_plane[:].bitcast(I32).rearrange("p (c w) -> p c w", c=CHUNKS)
+            for q in range(4):
+                nc.sync.dma_start(
+                    out=rows[32 * q : 32 * q + 4],
+                    in_=e_scales.bitcast(I32)[:, 4 * q : 4 * q + 4, :].rearrange("c r w -> r c w"),
+                )
+
+        def spread_beta(c, bank):
+            words = beta_words[:].bitcast(F32)
+            for u in range(2):
+                col = 2 * c + u
+                nc.tensor.transpose(bank[:, u * P : (u + 1) * P], words[:, col : col + 1].to_broadcast([P, P]), ident[:])
+            nc.scalar.copy(
+                out=beta_rows[c][:].bitcast(F32).rearrange("p (a u) -> p a u", u=2),
+                in_=bank[:, : 2 * P].rearrange("p (u a) -> p a u", u=2),
+            )
+
+        def turn(raw, bank):
+            words = raw[:].bitcast(F32)
+            for kk in range(2):
+                for u in range(2):
+                    col = (2 * kk + u) * P
+                    nc.tensor.transpose(bank[:, col : col + P], words[:, 2 * P * kk + u : 2 * P * (kk + 1) : 2], ident[:])
+
+        def unload_turned(engine, bank, laid):
+            copy_on(
+                engine,
+                laid.bitcast(F32).rearrange("p (s r u) -> p s r u", s=2, u=2),
+                bank[:].rearrange("p (s u r) -> p s r u", s=2, u=2),
+            )
+
+        def interleave(engine, src, dst, first, last):
+            cols = slice(first * P, last * P)
+            rows = src.rearrange("p (j n) -> p j n", j=PACK)[:, :, cols]
+            laid = dst.rearrange("p (n j) -> p n j", j=PACK)[:, cols, :]
+            if engine == "gpsimd":
+                copy_on(engine, laid, rows.rearrange("p j n -> p n j"))
+            else:
+                copy_on(
+                    engine,
+                    laid.rearrange("p (q i) j -> p q j i", i=4),
+                    rows.rearrange("p j (q i) -> p q j i", i=4),
+                )
+
+        def lay_w(engine, i, first=0, last=4):
+            interleave(engine, w_raw[i][:], w_laid[W_SLOT[i]][:], first, last)
+
+        def quantize_w(i):
+            quantize(w_codes[i], w_scales[i], w_laid[W_SLOT[i]])
+
+        def product(b, t, which, bank):
+            c, g = ORDER[b]
+            i = g * PACK + t
+            for kk in range(KPASSES):
+                w = piece(c, which, kk)
+                nc.tensor.matmul_mx(
+                    out=bank[:],
+                    lhsT=x_codes[i][:, kk * P : (kk + 1) * P].bitcast(FP8X4),
+                    lhsT_scale=x_scales[i][:, kk * P : (kk + 1) * P],
+                    rhs=w_codes[w][:].bitcast(FP8X4),
+                    rhs_scale=w_scales[w][:],
+                    start=(kk == 0),
+                    stop=(kk == KPASSES - 1),
+                )
+
+        def scale_advantage(b, t, bank):
+            c, g = ORDER[b]
+            i = g * PACK + t
+            nc.vector.scalar_tensor_tensor(
+                out=advantage[t][:],
+                in0=bank[:],
+                scalar=value_cols[:, i : i + 1],
+                in1=beta_rows[c][:],
+                op0=ALU.subtract,
+                op1=ALU.mult,
+            )
+
+        def add_policy(b, t, bank):
+            row = score[b % 3][:, t * PASS : (t + 1) * PASS]
+            nc.vector.tensor_tensor(
+                out=row.rearrange("p (u a e) -> p u a e", u=2, e=2),
+                in0=bank[:].rearrange("p (a u e) -> p u a e", u=2, e=2),
+                in1=advantage[t][:].rearrange("p (a u e) -> p u a e", u=2, e=2),
+                op=ALU.add,
+            )
+
+        def turn_score(b, pair, bank):
+            words = score[b % 3][:].bitcast(F32)
+            for s in range(4):
+                col = (4 * pair + s) * P
+                nc.tensor.transpose(bank[:, s * P : (s + 1) * P], words[:, col : col + P], ident[:])
+
+        def unload_score(engine, b, pair, bank):
+            unload_turned(engine, bank, by_token[b][:, pair * 2 * PASS : (pair + 1) * 2 * PASS])
+
+        def quantize_by_token(b):
+            quantize(tok_codes[b], tok_scales[b], by_token[b])
+
+        def quantize_token_pair(b, pair):
+            cols = slice(pair * 2 * P, (pair + 1) * 2 * P)
+            nc.vector.quantize_mx(
+                out=tok_codes[b][:, cols].bitcast(FP8X4),
+                scales=tok_scales[b][:, cols],
+                in_=by_token[b][:, pair * 2 * PASS : (pair + 1) * 2 * PASS],
+            )
+
+        def lay_by_context(engine, b, first=0, last=4):
+            interleave(engine, score[b % 3][:], by_context[b][:], first, last)
+
+        def quantize_by_context(b):
+            quantize(ctx_codes[b], ctx_scales[b], by_context[b])
+
+        def mixed_pass(c, i, g, bank):
+            b = ORDER.index((c, g))
+            nc.tensor.matmul_mx(
+                out=bank[:],
+                lhsT=mix_codes[i][:, g * P : (g + 1) * P].bitcast(FP8X4),
+                lhsT_scale=mix_scales[i][:, g * P : (g + 1) * P],
+                rhs=ctx_codes[b][:].bitcast(FP8X4),
+                rhs_scale=ctx_scales[b][:],
+                start=(g == 0),
+                stop=(g == GROUPS - 1),
+            )
+
+        def sketch_pass(g, t, c, bank):
+            b = ORDER.index((c, g))
+            nc.tensor.matmul_mx(
+                out=bank[:],
+                lhsT=tok_codes[b][:, t * P : (t + 1) * P].bitcast(FP8X4),
+                lhsT_scale=tok_scales[b][:, t * P : (t + 1) * P],
+                rhs=e_codes[:, c * 2 * D : (c + 1) * 2 * D].bitcast(FP4X4),
+                rhs_scale=e_plane[:, c * D : (c + 1) * D],
+                start=(c == 0),
+                stop=(c == CHUNKS - 1),
+            )
+
+        stored = []
+
+        def store_mixed(engine, c, i, bank):
+            out = result[len(stored) % 8]
+            stored.append(out)
+            copy_on(
+                engine,
+                out[:].rearrange("p (a u e) -> p a u e", u=2, e=2),
+                bank[:].rearrange("p (u a e) -> p a u e", u=2, e=2),
+            )
+            nc.sync.dma_start(out=mixed[i * P : (i + 1) * P, c * PASS : (c + 1) * PASS], in_=out[:])
+
+        def store_sketch(engine, g, t, bank):
+            out = result[len(stored) % 8]
+            stored.append(out)
+            copy_on(engine, out[:], bank[:])
+            nc.sync.dma_start(out=sketch_rows[g, t], in_=out[:])
+
+
+        ctx.enter_context(tc.manual_schedule())
+        load_small()
+        load_x(0)
+        load_w(0)
+        load_w(1)
+        for i in range(1, 4):
+            load_x(i)
+        load_w(2)
+        load_w(3)
+        for i in range(4, 8):
+            load_x(i)
+        for i in range(4, 8):
+            load_w(i)
+        make_identity(nc, ident[:])
+        nc.gpsimd.memset(e_plane[:].bitcast(I32), 0)
+
+        def turn_x(i, bank):
+            turn(x_raw[i], bank)
+            unload_turned("scalar", bank, half(X_HALF[i]))
+
+        def quantize_x(i):
+            quantize(x_codes[i], x_scales[i], half(X_HALF[i]))
+
+        def turn_mix(i, bank):
+            turn(mix_raw[i], bank)
+            unload_turned("scalar", bank, half(8 + i))
+
+        def quantize_mix(i):
+            quantize(mix_codes[i], mix_scales[i], half(8 + i))
+
+        def action(b, t):
+            product(b, t, 0, banks[t])
+            scale_advantage(b, t, banks[t])
+
+        def policy(b, t):
+            product(b, t, 1, banks[t])
+            add_policy(b, t, banks[t])
+
+        def actions(b):
+            for t in range(PACK):
+                action(b, t)
+
+        def policies(b):
+            for t in range(PACK):
+                policy(b, t)
+
+        def turn_block(b):
+            for pair in range(2):
+                turn_score(b, pair, banks[4 + pair])
+                unload_score("scalar", b, pair, banks[4 + pair])
+
+        def mixed_tile(c, i, bank, engine="scalar"):
+            for g in range(GROUPS):
+                mixed_pass(c, i, g, bank)
+            store_mixed(engine, c, i, bank)
+
+        def sketch_tile(g, t, bank, engine="scalar"):
+            for c in range(CHUNKS):
+                sketch_pass(g, t, c, bank)
+            store_sketch(engine, g, t, bank)
+
+        turn_x(0, banks[4])
+        for c in range(CHUNKS):
+            spread_beta(c, banks[5 + c])
+        lay_w("vector", 0, 0, 3)
+        lay_w("scalar", 0, 3, 4)
+        quantize_x(0)
+        quantize_w(0)
+        lay_w("scalar", 1, 2, 4)
+        lay_w("vector", 1, 0, 2)
+        for i in range(1, 4):
+            turn_x(i, banks[4 + i])
+        quantize_w(1)
+        quantize_x(1)
+        lay_w("vector", 2, 0, 2)
+        lay_w("scalar", 2, 2, 4)
+        action(0, 0)
+        quantize_x(2)
+        quantize_x(3)
+        lay_w("vector", 3, 0, 2)
+        lay_w("scalar", 3, 2, 4)
+        quantize_w(2)
+        action(0, 1)
+        quantize_w(3)
+        action(0, 2)
+        action(0, 3)
+        for i in range(4, 8):
+            turn_x(i, banks[i])
+        for i in range(RTILES):
+            load_mix(i)
+        for i in range(8, 12):
+            load_w(i)
+        load_e()
+        for i in range(4, 8):
+            quantize_x(i)
+        lay_w("gpsimd", 4)
+        lay_w("gpsimd", 5, 0, 2)
+        lay_w("scalar", 5, 2, 4)
+        policies(0)
+
+        lay_w("scalar", 6)
+        actions(1)
+        turn_block(0)
+        turn_mix(0, banks[6])
+        turn_mix(1, banks[7])
+        quantize_w(4)
+        quantize_w(5)
+        quantize_w(6)
+        lay_by_context("gpsimd", 0)
+        lay_w("gpsimd", 7, 0, 2)
+        lay_w("scalar", 7, 2, 4)
+        policies(1)
+        turn_mix(2, banks[6])
+        turn_mix(3, banks[7])
+        lay_by_context("scalar", 1)
+        actions(2)
+        turn_block(1)
+        quantize_w(7)
+        for i in range(RTILES):
+            quantize_mix(i)
+        quantize_by_context(0)
+        quantize_by_context(1)
+        lay_w("gpsimd", 8)
+        lay_w("gpsimd", 9, 0, 2)
+        lay_w("scalar", 9, 2, 4)
+        policies(2)
+        mixed_tile(0, 0, banks[6])
+        mixed_tile(0, 1, banks[7])
+        lay_w("scalar", 10)
+        actions(3)
+        turn_block(2)
+        quantize_w(8)
+        quantize_w(9)
+        quantize_w(10)
+        quantize_by_token(0)
+        mixed_tile(0, 2, banks[6])
+        mixed_tile(0, 3, banks[7])
+        lay_w("scalar", 11)
+        quantize_by_token(2)
+        policies(3)
+        quantize_w(11)
+        lay_by_context("scalar", 2)
+        lay_by_context("vector", 3, 0, 2)
+        lay_by_context("scalar", 3, 2, 4)
+        actions(4)
+        for t in range(2):
+            for c in range(2):
+                sketch_pass(0, t, c, banks[6 + t])
+        turn_block(3)
+        quantize_by_context(2)
+        quantize_by_context(3)
+        quantize_by_token(1)
+        policies(4)
+        mixed_tile(1, 0, banks[4])
+        mixed_tile(1, 1, banks[5])
+        actions(5)
+        turn_block(4)
+        lay_by_context("scalar", 4)
+        quantize_by_token(3)
+        quantize_by_token(4)
+        policies(5)
+        for t in range(2):
+            sketch_pass(0, t, 2, banks[6 + t])
+            store_sketch("scalar", 0, t, banks[6 + t])
+        mixed_tile(1, 2, banks[4])
+        mixed_tile(1, 3, banks[5])
+        quantize_by_context(4)
+
+        turn_score(5, 0, banks[6])
+        turn_score(5, 1, banks[7])
+        lay_by_context("vector", 5)
+        unload_score("scalar", 5, 0, banks[6])
+        unload_score("scalar", 5, 1, banks[7])
+        sketch_tile(0, 2, banks[0])
+        sketch_tile(0, 3, banks[1])
+        quantize_by_context(5)
+        quantize_by_token(5)
+        last = [banks[2], banks[3], banks[4], banks[5]]
+        for i in range(RTILES):
+            mixed_tile(2, i, last[i], ("vector", "scalar")[i % 2])
+        late = [banks[6], banks[7], banks[0], banks[1]]
+        for t in range(PACK):
+            sketch_tile(1, t, late[t], ("vector", "scalar")[t % 2])

@@ -23,8 +23,8 @@ CHUNKS = V // PASS
 KPASSES = K // PASS
 RTILES = R // P
 ORDER = [(0, 0), (0, 1), (1, 0), (1, 1), (2, 0), (2, 1)]
-W_SLOT = [0, 1, 2, 3, 1, 2, 3, 0, 1, 0, 2, 3]
-C_SLOT = [3, 1, 4, 5, 0, 1]
+W_SLOT = [0, 1, 2, 3, 1, 2, 3, 0, 1, 2, 3, 0]
+C_SLOT = [0, 1, 3, 5, 0, 1]
 X_HALF = [8, 9, 10, 11, 0, 1, 3, 2]
 
 
@@ -168,10 +168,10 @@ def tile_ilql_score_sketch_mix_s8_kernel(
         def quantize_w(i):
             quantize(w_codes[i], w_scales[i], w_laid[W_SLOT[i]])
 
-        def product(b, t, which, bank):
+        def product(b, t, which, bank, passes=range(KPASSES)):
             c, g = ORDER[b]
             i = g * PACK + t
-            for kk in range(KPASSES):
+            for kk in passes:
                 w = piece(c, which, kk)
                 nc.tensor.matmul_mx(
                     out=bank[:],
@@ -274,18 +274,23 @@ def tile_ilql_score_sketch_mix_s8_kernel(
 
 
         ctx.enter_context(tc.manual_schedule())
-        load_small()
-        load_x(0)
         load_w(0)
+        load_x(0)
+        load_small()
         load_w(1)
-        for i in range(1, 4):
-            load_x(i)
+        load_x(1)
+        load_x(2)
+        load_x(3)
         load_w(2)
         load_w(3)
-        for i in range(4, 8):
-            load_x(i)
-        for i in range(4, 8):
-            load_w(i)
+        load_x(4)
+        load_x(5)
+        load_x(6)
+        load_x(7)
+        load_w(4)
+        load_w(5)
+        load_w(6)
+        load_w(7)
         make_identity(nc, ident[:])
         nc.gpsimd.memset(e_plane[:].bitcast(I32), 0)
 
@@ -303,26 +308,26 @@ def tile_ilql_score_sketch_mix_s8_kernel(
         def quantize_mix(i):
             quantize(mix_codes[i], mix_scales[i], half(8 + i))
 
-        def action(b, t):
-            product(b, t, 0, banks[t])
-            scale_advantage(b, t, banks[t])
+        def action(b, t, bank):
+            product(b, t, 0, bank)
+            scale_advantage(b, t, bank)
 
-        def policy(b, t):
-            product(b, t, 1, banks[t])
-            add_policy(b, t, banks[t])
+        def policy(b, t, bank):
+            product(b, t, 1, bank)
+            add_policy(b, t, bank)
 
         def actions(b):
             for t in range(PACK):
-                action(b, t)
+                action(b, t, banks[t])
 
         def policies(b):
             for t in range(PACK):
-                policy(b, t)
+                policy(b, t, banks[t])
 
-        def turn_block(b):
+        def turn_block(b, first=4):
             for pair in range(2):
-                turn_score(b, pair, banks[4 + pair])
-                unload_score("scalar", b, pair, banks[4 + pair])
+                turn_score(b, pair, banks[first + pair])
+                unload_score("scalar", b, pair, banks[first + pair])
 
         def mixed_tile(c, i, bank, engine="scalar"):
             for g in range(GROUPS):
@@ -334,33 +339,35 @@ def tile_ilql_score_sketch_mix_s8_kernel(
                 sketch_pass(g, t, c, bank)
             store_sketch(engine, g, t, bank)
 
-        turn_x(0, banks[4])
-        for c in range(CHUNKS):
-            spread_beta(c, banks[5 + c])
         lay_w("vector", 0, 0, 3)
         lay_w("scalar", 0, 3, 4)
-        quantize_x(0)
+        for c in range(CHUNKS):
+            spread_beta(c, banks[5 + c])
+        turn_x(0, banks[4])
         quantize_w(0)
-        lay_w("scalar", 1, 2, 4)
         lay_w("vector", 1, 0, 2)
+        lay_w("scalar", 1, 2, 4)
+        quantize_x(0)
         for i in range(1, 4):
             turn_x(i, banks[4 + i])
         quantize_w(1)
         quantize_x(1)
+        quantize_x(2)
         lay_w("vector", 2, 0, 2)
         lay_w("scalar", 2, 2, 4)
-        action(0, 0)
-        quantize_x(2)
+        action(0, 0, banks[0])
         quantize_x(3)
         lay_w("vector", 3, 0, 2)
         lay_w("scalar", 3, 2, 4)
         quantize_w(2)
-        action(0, 1)
+        action(0, 1, banks[1])
         quantize_w(3)
-        action(0, 2)
-        action(0, 3)
-        for i in range(4, 8):
-            turn_x(i, banks[i])
+        action(0, 2, banks[2])
+        turn_x(4, banks[4])
+        turn_x(5, banks[5])
+        action(0, 3, banks[3])
+        turn_x(6, banks[6])
+        turn_x(7, banks[7])
         for i in range(RTILES):
             load_mix(i)
         for i in range(8, 12):
@@ -374,63 +381,72 @@ def tile_ilql_score_sketch_mix_s8_kernel(
         policies(0)
 
         lay_w("scalar", 6)
+        lay_w("scalar", 7)
         actions(1)
         turn_block(0)
-        turn_mix(0, banks[6])
-        turn_mix(1, banks[7])
         quantize_w(4)
         quantize_w(5)
         quantize_w(6)
+        quantize_w(7)
         lay_by_context("gpsimd", 0)
-        lay_w("gpsimd", 7, 0, 2)
-        lay_w("scalar", 7, 2, 4)
-        policies(1)
-        turn_mix(2, banks[6])
-        turn_mix(3, banks[7])
+        policy(1, 0, banks[0])
+        policy(1, 1, banks[1])
+        turn_mix(0, banks[6])
+        turn_mix(1, banks[7])
+        policy(1, 2, banks[2])
+        policy(1, 3, banks[3])
         lay_by_context("scalar", 1)
         actions(2)
         turn_block(1)
-        quantize_w(7)
-        for i in range(RTILES):
-            quantize_mix(i)
+        quantize_mix(0)
+        quantize_mix(1)
+        quantize_by_token(0)
         quantize_by_context(0)
         quantize_by_context(1)
         lay_w("gpsimd", 8)
         lay_w("gpsimd", 9, 0, 2)
         lay_w("scalar", 9, 2, 4)
-        policies(2)
-        mixed_tile(0, 0, banks[6])
-        mixed_tile(0, 1, banks[7])
+        policy(2, 0, banks[0])
+        policy(2, 1, banks[1])
+        turn_mix(2, banks[6])
+        turn_mix(3, banks[7])
+        policy(2, 2, banks[2])
+        policy(2, 3, banks[3])
+        mixed_tile(0, 0, banks[4])
+        mixed_tile(0, 1, banks[5])
         lay_w("scalar", 10)
         actions(3)
         turn_block(2)
+        quantize_mix(2)
+        quantize_mix(3)
         quantize_w(8)
+        quantize_by_token(2)
         quantize_w(9)
         quantize_w(10)
-        quantize_by_token(0)
-        mixed_tile(0, 2, banks[6])
-        mixed_tile(0, 3, banks[7])
+        lay_by_context("gpsimd", 2)
         lay_w("scalar", 11)
-        quantize_by_token(2)
         policies(3)
-        quantize_w(11)
-        lay_by_context("scalar", 2)
-        lay_by_context("vector", 3, 0, 2)
-        lay_by_context("scalar", 3, 2, 4)
-        actions(4)
+        mixed_tile(0, 2, banks[4])
+        mixed_tile(0, 3, banks[5])
         for t in range(2):
             for c in range(2):
                 sketch_pass(0, t, c, banks[6 + t])
+        lay_by_context("scalar", 3)
+        action(4, 0, banks[0])
+        action(4, 1, banks[1])
+        quantize_w(11)
+        action(4, 2, banks[2])
+        action(4, 3, banks[3])
         turn_block(3)
         quantize_by_context(2)
         quantize_by_context(3)
-        quantize_by_token(1)
         policies(4)
         mixed_tile(1, 0, banks[4])
         mixed_tile(1, 1, banks[5])
         actions(5)
         turn_block(4)
         lay_by_context("scalar", 4)
+        quantize_by_token(1)
         quantize_by_token(3)
         quantize_by_token(4)
         policies(5)
@@ -439,20 +455,24 @@ def tile_ilql_score_sketch_mix_s8_kernel(
             store_sketch("scalar", 0, t, banks[6 + t])
         mixed_tile(1, 2, banks[4])
         mixed_tile(1, 3, banks[5])
-        quantize_by_context(4)
+        sketch_tile(0, 2, banks[0])
 
         turn_score(5, 0, banks[6])
         turn_score(5, 1, banks[7])
         lay_by_context("vector", 5)
+        quantize_by_context(4)
         unload_score("scalar", 5, 0, banks[6])
         unload_score("scalar", 5, 1, banks[7])
-        sketch_tile(0, 2, banks[0])
         sketch_tile(0, 3, banks[1])
         quantize_by_context(5)
         quantize_by_token(5)
-        last = [banks[2], banks[3], banks[4], banks[5]]
+        for c in range(CHUNKS - 1):
+            sketch_pass(1, 0, c, banks[2])
+        last = [banks[3], banks[4], banks[5], banks[0]]
         for i in range(RTILES):
             mixed_tile(2, i, last[i], ("vector", "scalar")[i % 2])
-        late = [banks[6], banks[7], banks[0], banks[1]]
-        for t in range(PACK):
+        sketch_pass(1, 0, 2, banks[2])
+        store_sketch("vector", 1, 0, banks[2])
+        late = [banks[2], banks[6], banks[7], banks[1]]
+        for t in range(1, PACK):
             sketch_tile(1, t, late[t], ("vector", "scalar")[t % 2])

from contextlib import ExitStack

import concourse.mybir as mybir
from concourse.masks import make_identity

M, K, V, D, R = 1024, 1024, 1536, 512, 512
FLOPS = 2 * (2 * M * K * V + M * V * D + R * M * V)

F32 = mybir.dt.float32
BF16 = mybir.dt.bfloat16
I32 = mybir.dt.int32
U32 = mybir.dt.uint32
U8 = mybir.dt.uint8
FP8X4 = mybir.dt.float8_e4m3fn_x4
FP4X4 = mybir.dt.float4_e2m1fn_x4
ALU = mybir.AluOpType

P = 128
PACK = 4
PASS = P * PACK
GROUPS = M // PASS
CHUNKS = V // PASS
KPASSES = K // PASS
RTILES = R // P
ORDER = [(0, 0), (0, 1), (1, 0), (1, 1), (2, 0), (2, 1)]
W_SLOT = [0, 1, 2, 3, 1, 2, 3, 0, 1, 2, 3, 0]
C_SLOT = [0, 1, 3, 5, 0, 1]
X_HALF = [8, 9, 10, 11, 0, 1, 3, 2]


def tile_ilql_score_sketch_mix_s8_kernel(
    tc, x, w_pi, w_act, beta, values, e_words, e_scales, mix, sketch, mixed
):
    nc = tc.nc
    with ExitStack() as ctx:
        sb = ctx.enter_context(tc.tile_pool(name="sb", bufs=1))
        ps = ctx.enter_context(tc.psum_pool(name="ps", bufs=1))

        def tiles(name, count, width, dtype):
            return [sb.tile([P, width], dtype, name="%s%d" % (name, i), align_bytes=64) for i in range(count)]

        banks = [ps.tile([P, PASS], F32, name="bank%d" % i) for i in range(8)]

        ident = sb.tile([P, P], F32, name="ident")
        beta_words = sb.tile([P, CHUNKS * PACK], BF16, name="beta_words")
        value_cols = sb.tile([P, GROUPS * PACK], BF16, name="value_cols")
        beta_rows = tiles("beta_rows", CHUNKS, PASS, BF16)
        x_raw = tiles("x_raw", GROUPS * PACK, K, BF16)
        x_codes = tiles("x_codes", GROUPS * PACK, KPASSES * P, U32)
        x_scales = tiles("x_scales", GROUPS * PACK, KPASSES * P, U8)
        mix_raw = x_raw[:RTILES]
        mix_codes = tiles("mix_codes", RTILES, GROUPS * P, U32)
        mix_scales = tiles("mix_scales", RTILES, GROUPS * P, U8)
        n_pieces = CHUNKS * 2 * KPASSES
        w_raw = tiles("w_raw", n_pieces, PACK * PASS, BF16)
        w_laid = tiles("w_laid", 6, PACK * PASS, BF16)
        w_codes = tiles("w_codes", n_pieces, PASS, U32)
        w_scales = tiles("w_scales", n_pieces, PASS, U8)
        e_codes = sb.tile([P, CHUNKS * 2 * D], U8, name="e_codes", align_bytes=64)
        e_plane = sb.tile([P, CHUNKS * D], U8, name="e_plane", align_bytes=64)
        advantage = tiles("advantage", 4, PASS, F32)
        score = tiles("score", 3, PACK * PASS, BF16)
        by_token = w_raw
        by_context = [w_laid[s] for s in C_SLOT]
        n_blocks = CHUNKS * GROUPS
        tok_codes = tiles("tok_codes", n_blocks, PASS, U32)
        tok_scales = tiles("tok_scales", n_blocks, PASS, U8)
        ctx_codes = tiles("ctx_codes", n_blocks, PASS, U32)
        ctx_scales = tiles("ctx_scales", n_blocks, PASS, U8)
        result = tiles("result", 8, PASS, F32)

        def copy_on(engine, out, in_):
            if engine == "vector":
                nc.vector.tensor_copy(out=out, in_=in_)
            elif engine == "scalar":
                nc.scalar.copy(out=out, in_=in_)
            else:
                nc.gpsimd.tensor_scalar(out=out, in0=in_, scalar1=1.0, scalar2=0.0, op0=ALU.mult, op1=ALU.add)

        def quantize(codes, scales, laid):
            nc.vector.quantize_mx(out=codes[:].bitcast(FP8X4), scales=scales[:], in_=laid[:])

        def half(h):
            return w_laid[h // 2][:, (h % 2) * K : (h % 2 + 1) * K]

        x_rows = x.rearrange("(g p t) k -> g t p k", p=P, t=PACK)
        sketch_rows = sketch.rearrange("(g p t) d -> g t p d", p=P, t=PACK)

        def load_x(i):
            nc.sync.dma_start(out=x_raw[i][:], in_=x_rows[i // PACK, i % PACK])

        def load_mix(i):
            nc.sync.dma_start(out=mix_raw[i][:], in_=mix[i * P : (i + 1) * P, :])

        def piece(c, which, kk):
            return (c * 2 + which) * KPASSES + kk

        def load_w(i):
            c, which, kk = i // (2 * KPASSES), (i // KPASSES) % 2, i % KPASSES
            src = (w_act, w_pi)[which][kk * PASS : (kk + 1) * PASS, c * PASS : (c + 1) * PASS]
            nc.sync.dma_start(
                out=w_raw[i][:].rearrange("p (j n) -> p j n", j=PACK),
                in_=src.rearrange("(p j) n -> p j n", j=PACK),
            )

        def load_small():
            nc.scalar.dma_start(
                out=beta_words[:].rearrange("a (c f) -> a c f", f=PACK),
                in_=beta.rearrange("(c a f) -> a c f", a=P, f=PACK),
            )
            nc.scalar.dma_start(
                out=value_cols[:].rearrange("p (g t) -> p g t", t=PACK),
                in_=values.rearrange("(g p t) -> p g t", p=P, t=PACK),
            )

        def load_e():
            nc.sync.dma_start(
                out=e_codes[:].bitcast(I32).rearrange("p (c w) -> p c w", c=CHUNKS),
                in_=e_words.bitcast(I32).rearrange("c p w -> p c w"),
            )
            rows = e_plane[:].bitcast(I32).rearrange("p (c w) -> p c w", c=CHUNKS)
            for q in range(4):
                nc.sync.dma_start(
                    out=rows[32 * q : 32 * q + 4],
                    in_=e_scales.bitcast(I32)[:, 4 * q : 4 * q + 4, :].rearrange("c r w -> r c w"),
                )

        def spread_beta(c, bank):
            words = beta_words[:].bitcast(F32)
            for u in range(2):
                col = 2 * c + u
                nc.tensor.transpose(bank[:, u * P : (u + 1) * P], words[:, col : col + 1].to_broadcast([P, P]), ident[:])
            nc.scalar.copy(
                out=beta_rows[c][:].bitcast(F32).rearrange("p (a u) -> p a u", u=2),
                in_=bank[:, : 2 * P].rearrange("p (u a) -> p a u", u=2),
            )

        def turn(raw, bank):
            words = raw[:].bitcast(F32)
            for kk in range(2):
                for u in range(2):
                    col = (2 * kk + u) * P
                    nc.tensor.transpose(bank[:, col : col + P], words[:, 2 * P * kk + u : 2 * P * (kk + 1) : 2], ident[:])

        def unload_turned(engine, bank, laid):
            copy_on(
                engine,
                laid.bitcast(F32).rearrange("p (s r u) -> p s r u", s=2, u=2),
                bank[:].rearrange("p (s u r) -> p s r u", s=2, u=2),
            )

        def interleave(engine, src, dst, first, last):
            cols = slice(first * P, last * P)
            rows = src.rearrange("p (j n) -> p j n", j=PACK)[:, :, cols]
            laid = dst.rearrange("p (n j) -> p n j", j=PACK)[:, cols, :]
            if engine == "gpsimd":
                copy_on(engine, laid, rows.rearrange("p j n -> p n j"))
            else:
                copy_on(
                    engine,
                    laid.rearrange("p (q i) j -> p q j i", i=4),
                    rows.rearrange("p j (q i) -> p q j i", i=4),
                )

        def lay_w(engine, i, first=0, last=4):
            interleave(engine, w_raw[i][:], w_laid[W_SLOT[i]][:], first, last)

        def quantize_w(i):
            quantize(w_codes[i], w_scales[i], w_laid[W_SLOT[i]])

        def product(b, t, which, bank, passes=range(KPASSES)):
            c, g = ORDER[b]
            i = g * PACK + t
            for kk in passes:
                w = piece(c, which, kk)
                nc.tensor.matmul_mx(
                    out=bank[:],
                    lhsT=x_codes[i][:, kk * P : (kk + 1) * P].bitcast(FP8X4),
                    lhsT_scale=x_scales[i][:, kk * P : (kk + 1) * P],
                    rhs=w_codes[w][:].bitcast(FP8X4),
                    rhs_scale=w_scales[w][:],
                    start=(kk == 0),
                    stop=(kk == KPASSES - 1),
                )

        def scale_advantage(b, t, bank):
            c, g = ORDER[b]
            i = g * PACK + t
            nc.vector.scalar_tensor_tensor(
                out=advantage[t][:],
                in0=bank[:],
                scalar=value_cols[:, i : i + 1],
                in1=beta_rows[c][:],
                op0=ALU.subtract,
                op1=ALU.mult,
            )

        def add_policy(b, t, bank):
            row = score[b % 3][:, t * PASS : (t + 1) * PASS]
            nc.vector.tensor_tensor(
                out=row.rearrange("p (u a e) -> p u a e", u=2, e=2),
                in0=bank[:].rearrange("p (a u e) -> p u a e", u=2, e=2),
                in1=advantage[t][:].rearrange("p (a u e) -> p u a e", u=2, e=2),
                op=ALU.add,
            )

        def turn_score(b, pair, bank):
            words = score[b % 3][:].bitcast(F32)
            for s in range(4):
                col = (4 * pair + s) * P
                nc.tensor.transpose(bank[:, s * P : (s + 1) * P], words[:, col : col + P], ident[:])

        def unload_score(engine, b, pair, bank):
            unload_turned(engine, bank, by_token[b][:, pair * 2 * PASS : (pair + 1) * 2 * PASS])

        def quantize_by_token(b):
            quantize(tok_codes[b], tok_scales[b], by_token[b])

        def quantize_token_pair(b, pair):
            cols = slice(pair * 2 * P, (pair + 1) * 2 * P)
            nc.vector.quantize_mx(
                out=tok_codes[b][:, cols].bitcast(FP8X4),
                scales=tok_scales[b][:, cols],
                in_=by_token[b][:, pair * 2 * PASS : (pair + 1) * 2 * PASS],
            )

        def lay_by_context(engine, b, first=0, last=4):
            interleave(engine, score[b % 3][:], by_context[b][:], first, last)

        def quantize_by_context(b):
            quantize(ctx_codes[b], ctx_scales[b], by_context[b])

        def mixed_pass(c, i, g, bank):
            b = ORDER.index((c, g))
            nc.tensor.matmul_mx(
                out=bank[:],
                lhsT=mix_codes[i][:, g * P : (g + 1) * P].bitcast(FP8X4),
                lhsT_scale=mix_scales[i][:, g * P : (g + 1) * P],
                rhs=ctx_codes[b][:].bitcast(FP8X4),
                rhs_scale=ctx_scales[b][:],
                start=(g == 0),
                stop=(g == GROUPS - 1),
            )

        def sketch_pass(g, t, c, bank):
            b = ORDER.index((c, g))
            nc.tensor.matmul_mx(
                out=bank[:],
                lhsT=tok_codes[b][:, t * P : (t + 1) * P].bitcast(FP8X4),
                lhsT_scale=tok_scales[b][:, t * P : (t + 1) * P],
                rhs=e_codes[:, c * 2 * D : (c + 1) * 2 * D].bitcast(FP4X4),
                rhs_scale=e_plane[:, c * D : (c + 1) * D],
                start=(c == 0),
                stop=(c == CHUNKS - 1),
            )

        stored = []

        def store_mixed(engine, c, i, bank):
            out = result[len(stored) % 8]
            stored.append(out)
            copy_on(
                engine,
                out[:].rearrange("p (a u e) -> p a u e", u=2, e=2),
                bank[:].rearrange("p (u a e) -> p a u e", u=2, e=2),
            )
            nc.sync.dma_start(out=mixed[i * P : (i + 1) * P, c * PASS : (c + 1) * PASS], in_=out[:])

        def store_sketch(engine, g, t, bank):
            out = result[len(stored) % 8]
            stored.append(out)
            copy_on(engine, out[:], bank[:])
            nc.sync.dma_start(out=sketch_rows[g, t], in_=out[:])


        ctx.enter_context(tc.manual_schedule())
        load_w(0)
        load_x(0)
        load_small()
        load_w(1)
        load_x(1)
        load_x(2)
        load_x(3)
        load_w(2)
        load_w(3)
        load_x(4)
        load_x(5)
        load_x(6)
        load_x(7)
        load_w(4)
        load_w(5)
        load_w(6)
        load_w(7)
        make_identity(nc, ident[:])
        nc.gpsimd.memset(e_plane[:].bitcast(I32), 0)

        def turn_x(i, bank):
            turn(x_raw[i], bank)
            unload_turned("scalar", bank, half(X_HALF[i]))

        def quantize_x(i):
            quantize(x_codes[i], x_scales[i], half(X_HALF[i]))

        def turn_mix(i, bank):
            turn(mix_raw[i], bank)
            unload_turned("scalar", bank, half(8 + i))

        def quantize_mix(i):
            quantize(mix_codes[i], mix_scales[i], half(8 + i))

        def action(b, t, bank):
            product(b, t, 0, bank)
            scale_advantage(b, t, bank)

        def policy(b, t, bank):
            product(b, t, 1, bank)
            add_policy(b, t, bank)

        def actions(b):
            for t in range(PACK):
                action(b, t, banks[t])

        def policies(b):
            for t in range(PACK):
                policy(b, t, banks[t])

        def turn_block(b, first=4):
            for pair in range(2):
                turn_score(b, pair, banks[first + pair])
                unload_score("scalar", b, pair, banks[first + pair])

        def mixed_tile(c, i, bank, engine="scalar"):
            for g in range(GROUPS):
                mixed_pass(c, i, g, bank)
            store_mixed(engine, c, i, bank)

        def sketch_tile(g, t, bank, engine="scalar"):
            for c in range(CHUNKS):
                sketch_pass(g, t, c, bank)
            store_sketch(engine, g, t, bank)

        lay_w("vector", 0, 0, 3)
        lay_w("scalar", 0, 3, 4)
        for c in range(CHUNKS):
            spread_beta(c, banks[5 + c])
        turn_x(0, banks[4])
        quantize_w(0)
        lay_w("vector", 1, 0, 2)
        lay_w("scalar", 1, 2, 4)
        quantize_x(0)
        for i in range(1, 4):
            turn_x(i, banks[4 + i])
        quantize_w(1)
        quantize_x(1)
        quantize_x(2)
        lay_w("vector", 2, 0, 2)
        lay_w("scalar", 2, 2, 4)
        action(0, 0, banks[0])
        quantize_x(3)
        lay_w("vector", 3, 0, 2)
        lay_w("scalar", 3, 2, 4)
        quantize_w(2)
        action(0, 1, banks[1])
        quantize_w(3)
        action(0, 2, banks[2])
        turn_x(4, banks[4])
        turn_x(5, banks[5])
        action(0, 3, banks[3])
        turn_x(6, banks[6])
        turn_x(7, banks[7])
        for i in range(RTILES):
            load_mix(i)
        for i in range(8, 12):
            load_w(i)
        load_e()
        for i in range(4, 8):
            quantize_x(i)
        lay_w("gpsimd", 4)
        lay_w("gpsimd", 5, 0, 2)
        lay_w("scalar", 5, 2, 4)
        policies(0)

        lay_w("scalar", 6)
        lay_w("scalar", 7)
        actions(1)
        turn_block(0)
        quantize_w(4)
        quantize_w(5)
        quantize_w(6)
        quantize_w(7)
        lay_by_context("gpsimd", 0)
        policy(1, 0, banks[0])
        policy(1, 1, banks[1])
        turn_mix(0, banks[6])
        turn_mix(1, banks[7])
        policy(1, 2, banks[2])
        policy(1, 3, banks[3])
        lay_by_context("scalar", 1)
        actions(2)
        turn_block(1)
        quantize_mix(0)
        quantize_mix(1)
        quantize_by_token(0)
        quantize_by_context(0)
        quantize_by_context(1)
        lay_w("gpsimd", 8)
        lay_w("gpsimd", 9, 0, 2)
        lay_w("scalar", 9, 2, 4)
        policy(2, 0, banks[0])
        policy(2, 1, banks[1])
        turn_mix(2, banks[6])
        turn_mix(3, banks[7])
        policy(2, 2, banks[2])
        policy(2, 3, banks[3])
        mixed_tile(0, 0, banks[4])
        mixed_tile(0, 1, banks[5])
        lay_w("scalar", 10)
        actions(3)
        turn_block(2)
        quantize_mix(2)
        quantize_mix(3)
        quantize_w(8)
        quantize_by_token(2)
        quantize_w(9)
        quantize_w(10)
        lay_by_context("gpsimd", 2)
        lay_w("scalar", 11)
        policies(3)
        mixed_tile(0, 2, banks[4])
        mixed_tile(0, 3, banks[5])
        for t in range(2):
            for c in range(2):
                sketch_pass(0, t, c, banks[6 + t])
        lay_by_context("scalar", 3)
        action(4, 0, banks[0])
        action(4, 1, banks[1])
        quantize_w(11)
        action(4, 2, banks[2])
        action(4, 3, banks[3])
        turn_block(3)
        quantize_by_context(2)
        quantize_by_context(3)
        policies(4)
        mixed_tile(1, 0, banks[4])
        mixed_tile(1, 1, banks[5])
        actions(5)
        turn_block(4)
        lay_by_context("scalar", 4)
        quantize_by_token(1)
        quantize_by_token(3)
        quantize_by_token(4)
        policies(5)
        for t in range(2):
            sketch_pass(0, t, 2, banks[6 + t])
            store_sketch("scalar", 0, t, banks[6 + t])
        mixed_tile(1, 2, banks[4])
        mixed_tile(1, 3, banks[5])
        sketch_tile(0, 2, banks[0])

        turn_score(5, 0, banks[6])
        turn_score(5, 1, banks[7])
        lay_by_context("vector", 5)
        quantize_by_context(4)
        unload_score("scalar", 5, 0, banks[6])
        unload_score("scalar", 5, 1, banks[7])
        sketch_tile(0, 3, banks[1])
        quantize_by_context(5)
        quantize_by_token(5)
        for c in range(CHUNKS - 1):
            sketch_pass(1, 0, c, banks[2])
        last = [banks[3], banks[4], banks[5], banks[0]]
        for i in range(RTILES):
            mixed_tile(2, i, last[i], ("vector", "scalar")[i % 2])
        sketch_pass(1, 0, 2, banks[2])
        store_sketch("vector", 1, 0, banks[2])
        late = [banks[2], banks[6], banks[7], banks[1]]
        for t in range(1, PACK):
            sketch_tile(1, t, late[t], ("vector", "scalar")[t % 2])
